import numpy as np
import ml_dtypes


def mxq(x, axis, fmt="e4m3"):
    dtype, down = {"e4m3": (ml_dtypes.float8_e4m3fn, 7), "e5m2": (ml_dtypes.float8_e5m2, 14)}[fmt]
    v = np.moveaxis(np.asarray(x, np.float32).astype(ml_dtypes.bfloat16).astype(np.float64), axis, -1)
    blocks = v.reshape(v.shape[:-1] + (-1, 32))
    amax = np.abs(blocks).max(-1, keepdims=True)
    byte = np.maximum(np.where(amax > 0, np.frexp(amax)[1] - 1 + 127, 0) - down, 1)
    scale = np.exp2(byte - 127.0)
    codes = (blocks / scale).astype(np.float32).astype(dtype).astype(np.float64)
    return np.moveaxis((codes * scale).reshape(v.shape), -1, axis)


WIDE = False


def mx_kscale(k):
    if not WIDE:
        return np.ones(k)
    levels = np.array([10, -10, 5, -5, 0])
    if k % 512:
        return np.exp2(np.random.permutation(np.resize(levels, k // 32))).repeat(32)
    a = np.empty((k // 512, 16))
    for p in range(k // 512):
        a[p, :8] = np.random.permutation(np.resize(levels, 8))
        for g in range(8):
            far = levels[np.abs(levels - a[p, g]) >= 10]
            a[p, g + 8] = far[np.random.randint(len(far))]
    return np.exp2(a.ravel()).repeat(32)


def f64(x):
    return np.asarray(x).astype(np.float64)


def striped(idx):
    return np.tile(np.asarray(idx).reshape(-1, 16).T, (8, 1)).astype(np.uint16)


def unstriped(offs):
    return offs[:16].T.reshape(-1).astype(np.int64)


E2M1 = np.array([0.0, 0.5, 1.0, 1.5, 2.0, 3.0, 4.0, 6.0, -0.0, -0.5, -1.0, -1.5, -2.0, -3.0, -4.0, -6.0])


def pack_weight(w, fmt):
    k, n = w.shape
    w = f64(np.asarray(w, np.float32).astype(ml_dtypes.bfloat16)).reshape(k // 32, 32, n)
    amax = np.abs(w).max(1)
    if fmt == "e4m3":
        byte = np.frexp(amax)[1] - 1 + 127 - 7
    else:
        mant, ex = np.frexp(amax / 6.0)
        byte = np.where(mant > 0.5, ex, ex - 1) + 127
    byte = np.clip(np.where(amax > 0, byte, 1), 1, 254)
    scaled = (w * np.exp2(127.0 - byte)[:, None, :]).reshape(k, n).astype(np.float32)
    by_word = np.ascontiguousarray(scaled.reshape(k // 512, 128, 4, n).transpose(0, 1, 3, 2))
    if fmt == "e4m3":
        words = by_word.astype(ml_dtypes.float8_e4m3fn).view(np.uint8)
    else:
        c = by_word.astype(ml_dtypes.float4_e2m1fn).view(np.uint8) & 0xF
        words = (c[..., 0::2] | (c[..., 1::2] << 4)).reshape(k // 512, 128, 2 * n)
    return np.ascontiguousarray(words), np.ascontiguousarray(byte.astype(np.uint8).reshape(k // 512, 16, n))


def unpack_weight(words, scales, fmt):
    g, _, n = scales.shape
    words = np.ascontiguousarray(words).reshape(g, 128, n, -1)
    if fmt == "e4m3":
        vals = words.view(ml_dtypes.float8_e4m3fn).astype(np.float64)
    else:
        nib = np.empty((g, 128, n, 4), np.uint8)
        nib[..., 0::2] = words & 0xF
        nib[..., 1::2] = words >> 4
        vals = E2M1[nib]
    vals = vals * np.repeat(np.exp2(scales.astype(np.float64) - 127.0), 8, axis=1)[..., None]
    return vals.transpose(0, 1, 3, 2).reshape(g * 512, n)


def softplus(v):
    return np.log(1.0 + np.exp(v))


def sigmoid(v):
    return 1.0 / (1.0 + np.exp(-v))


D, E, T, I, Q = 512, 512, 2048, 512, 128


def setup_inputs():
    n = np.random.standard_normal
    idx = np.random.permutation(T)[:I]
    fd = mx_kscale(D)
    fe = mx_kscale(E)
    keysp = pack_weight(n((D, T)) / fd[:, None], "e4m3")
    valsp = pack_weight(n((E, T)) / fe[:, None], "e4m3")
    return {
        "query": (n((D, Q)) * 1.0 / np.sqrt(D) * fd[:, None]).astype(np.float32),
        "keys_words": keysp[0],
        "keys_scales": keysp[1],
        "th": (np.random.uniform(-0.5, 0.5, (Q, 1))).astype(np.float32),
        "reserve": (np.random.uniform(20.0, 100.0, (Q, 1))).astype(np.float32),
        "gout": (n((E, Q)) * 1 / np.sqrt(E) * fe[:, None]).astype(np.float32),
        "vals_words": valsp[0],
        "vals_scales": valsp[1],
        "size": (np.random.uniform(0.5, 2.0, (1, I))).astype(np.float32),
        "dquery": (n((D, Q)) * 1.0 / np.sqrt(D) * fd[:, None]).astype(np.float32),
        "base": (0.5 * n((Q, T))).astype(np.float32),
        "offs": striped(idx),
    }


def reference(query, keys_words, keys_scales, th, reserve, gout, vals_words, vals_scales, size, dquery, base, offs):
    idx = unstriped(offs)
    keysu = unpack_weight(keys_words, keys_scales, "e4m3")
    valsu = unpack_weight(vals_words, vals_scales, "e4m3")
    queryq = mxq(f64(query), 0, "e4m3")
    keysidxg = keysu[:, idx]
    a = queryq.T @ keysidxg
    dqueryq = mxq(f64(dquery), 0, "e4m3")
    ta = dqueryq.T @ keysidxg
    p = softplus(a - f64(th))
    z = np.sum(p, axis=1, keepdims=True) + f64(reserve)
    goutq = mxq(f64(gout), 0, "e4m3")
    valsidxg = valsu[:, idx]
    c0 = goutq.T @ valsidxg
    dz = np.sum(c0 * p * f64(size) / np.square(z) * (-1.0), axis=1, keepdims=True)
    dp = c0 / z * f64(size) + dz
    tp = ta * sigmoid(a - f64(th))
    tz = np.sum(tp, axis=1, keepdims=True)
    tdz = np.sum((tp * f64(size) * c0 - tz * z * 2.0 * c0 * p * f64(size) / np.square(z)) / np.square(z) * (-1.0), axis=1, keepdims=True)
    tdp = tz * c0 / np.square(z) * (-1.0) * f64(size) + tdz
    tda = tdp * sigmoid(a - f64(th)) + ta * sigmoid(a - f64(th)) * (1.0 - sigmoid(a - f64(th))) * dp
    gs = tda * 512.0
    gf = np.zeros((Q, T))
    gf[:, idx] = gs
    y = f64(base) + gf
    return y

@@ -1,0 +1,185 @@
+from contextlib import ExitStack
+
+import concourse.mybir as mybir
+from concourse.masks import make_identity
+
+F32 = mybir.dt.float32
+BF16 = mybir.dt.bfloat16
+I32 = mybir.dt.int32
+U32 = mybir.dt.uint32
+U16 = mybir.dt.uint16
+U8 = mybir.dt.uint8
+FP8X4 = mybir.dt.float8_e4m3fn_x4
+ALU = mybir.AluOpType
+ACT = mybir.ActivationFunctionType
+
+P = 128
+PACK = 4
+TOKENS = 2048
+SLOTS = 512
+ROWS = 128
+GAIN = 512.0
+OUT_CHUNKS = (256, 512, 512, 512, 256)
+
+FLOPS = 3 * 2 * 512 * ROWS * SLOTS
+
+
+def tile_attend_hvsoftthreshold_s_kernel(tc, query, keys_words, keys_scales, th, reserve, gout,
+                                          vals_words, vals_scales, size, dquery, base, offs, out):
+    nc = tc.nc
+    with ExitStack() as ctx:
+        held = ctx.enter_context(tc.tile_pool(name="held", bufs=1))
+        psum = ctx.enter_context(tc.psum_pool(name="psum", bufs=1))
+
+        def big(name, tag=None):
+            return held.tile([P, SLOTS], F32, name=name, tag=tag or name)
+
+        def col(name, tag=None):
+            return held.tile([P, 1], F32, name=name, tag=tag or name)
+
+        offsets = held.tile([P, SLOTS // 16], U16, name="offsets")
+        nc.sync.dma_start(offsets[:], offs)
+
+        def scale_pool(name, scales):
+            t = held.tile([P, TOKENS], U8, name=name)
+            nc.vector.memset(t[:].bitcast(I32), 0)
+            for quad in range(4):
+                nc.sync.dma_start(out=t[32 * quad:32 * quad + 4, :].bitcast(I32),
+                                  in_=scales[0, 4 * quad:4 * quad + 4, :].bitcast(I32))
+            return t
+
+        def word_pool(name, words):
+            t = held.tile([P, TOKENS], U32, name=name)
+            nc.sync.dma_start(out=t[:].bitcast(I32), in_=words[0].rearrange("p n t -> p (n t)").bitcast(I32))
+            return t
+
+        def load_rows(name, x):
+            t = held.tile([P, PACK, ROWS], F32, name=name)
+            nc.sync.dma_start(out=t[:], in_=x.rearrange("(p j) w -> p j w", j=PACK))
+            return t
+
+        zero = col("zero")
+        nc.gpsimd.memset(zero[:], 0.0)
+        half = col("half")
+        nc.scalar.activation(half[:], zero[:], ACT.Sigmoid)
+
+        identity = held.tile([P, P], F32, name="identity")
+        make_identity(nc, identity[:])
+        size_cols = held.tile([P, PACK], F32, name="size_cols")
+        nc.sync.dma_start(out=size_cols[:], in_=size.rearrange("o (p j) -> (o p) j", j=PACK))
+        th_sb = col("th_sb")
+        nc.gpsimd.dma_start(out=th_sb[:], in_=th)
+
+        query_raw = load_rows("query_raw", query)
+        key_scale_pool = scale_pool("key_scale_pool", keys_scales)
+        key_word_pool = word_pool("key_word_pool", keys_words)
+        dquery_raw = load_rows("dquery_raw", dquery)
+        val_scale_pool = scale_pool("val_scale_pool", vals_scales)
+        gout_raw = load_rows("gout_raw", gout)
+        val_word_pool = word_pool("val_word_pool", vals_words)
+        reserve_sb = col("reserve_sb")
+        nc.sync.dma_start(out=reserve_sb[:], in_=reserve)
+        base_sb = held.tile([P, TOKENS], F32, name="base_sb")
+        nc.sync.dma_start(out=base_sb[:], in_=base)
+
+        neg_th = col("neg_th")
+        nc.gpsimd.tensor_scalar(neg_th[:], th_sb[:], -1.0, 0.0, ALU.mult, ALU.add)
+
+        placed = held.tile([P, TOKENS], F32, name="placed")
+        nc.vector.memset(placed[:], 0.0)
+
+        size_ps = psum.tile([P, PACK, P], F32, name="size_ps")
+        for j in range(PACK):
+            nc.tensor.transpose(size_ps[:, j, :], size_cols[:, j:j + 1].to_broadcast([P, P]), identity[:])
+        size_rows = big("size_rows")
+        nc.scalar.copy(out=size_rows[:].rearrange("p (n j) -> p n j", j=PACK),
+                       in_=size_ps[:].rearrange("p j n -> p n j"))
+
+        def gather(name, pool, dtype, tag=None):
+            t = held.tile([P, SLOTS], dtype, name=name, tag=tag or name, align_bytes=64)
+            nc.vector.tensor_copy(t[:], pool[:].indirect(offsets[:]))
+            return t
+
+        def quantise(name, raw):
+            grouped = held.tile([P, ROWS, PACK], BF16, name=name + "_bf16", align_bytes=64)
+            nc.scalar.copy(out=grouped[:], in_=raw[:].rearrange("p j w -> p w j"))
+            words = held.tile([P, ROWS], U32, name=name + "_words", align_bytes=64)
+            scales = held.tile([P, ROWS], U8, name=name + "_scales", align_bytes=64)
+            nc.vector.quantize_mx(out=words[:].bitcast(FP8X4), scales=scales[:],
+                                  in_=grouped[:].rearrange("p w j -> p (w j)"))
+            return words, scales
+
+        def product(name, rows, words, scales, tag=None):
+            acc = psum.tile([P, SLOTS], F32, name=name, tag=tag or name)
+            nc.tensor.matmul_mx(out=acc[:], lhsT=rows[0][:].bitcast(FP8X4), lhsT_scale=rows[1][:],
+                                rhs=words[:].bitcast(FP8X4), rhs_scale=scales[:], start=True, stop=True)
+            return acc
+
+        key_scales = gather("key_scales", key_scale_pool, U8)
+        query_mx = quantise("query", query_raw)
+        key_words = gather("key_words", key_word_pool, U32)
+        a = product("a", query_mx, key_words, key_scales, tag="size_ps")
+        ta = product("ta", quantise("dquery", dquery_raw), key_words, key_scales)
+        val_scales = gather("val_scales", val_scale_pool, U8, tag="dquery_bf16")
+
+        gout_mx = quantise("gout", gout_raw)
+        s = big("s", tag="gout_raw")
+        nc.scalar.activation(s[:], a[:], ACT.Sigmoid, bias=neg_th[:])
+        dist = big("dist")
+        nc.scalar.activation(dist[:], s[:], ACT.Abs, bias=half[:], scale=-1.0)
+        log_m = big("log_m")
+        sum_log_m = col("sum_log_m")
+        nc.scalar.activation(log_m[:], dist[:], ACT.Ln, bias=half[:], accum_out=sum_log_m[:])
+        relu_x = big("relu_x", tag="dist")
+        sum_relu_x = col("sum_relu_x")
+        nc.scalar.activation(relu_x[:], a[:], ACT.Relu, bias=neg_th[:], accum_out=sum_relu_x[:])
+
+        neg_tp = big("neg_tp", tag="val_scale_pool")
+        neg_tz = col("neg_tz")
+        nc.vector.scalar_tensor_tensor(neg_tp[:], ta[:], -1.0, s[:], ALU.mult, ALU.mult, accum_out=neg_tz[:])
+
+        val_words = gather("val_words", val_word_pool, U32)
+        c0 = product("c0", gout_mx, val_words, val_scales)
+        neg_v = big("neg_v", tag="val_word_pool")
+        nc.vector.scalar_tensor_tensor(neg_v[:], s[:], 1.0, ta[:], ALU.subtract, ALU.mult)
+        u = big("u")
+        nc.vector.tensor_tensor(u[:], c0[:], size_rows[:], ALU.mult)
+        z = held.tile([P, 1], F32, name="z", tag="dquery_bf16", align_bytes=64)
+        nc.vector.tensor_scalar(z[:], sum_relu_x[:], sum_log_m[:], reserve_sb[:], ALU.subtract, ALU.add)
+        neg_p = held.tile([P, SLOTS], F32, name="neg_p", tag="val_words", align_bytes=64)
+        nc.vector.tensor_tensor(neg_p[:], log_m[:], relu_x[:], ALU.subtract)
+        r = col("r")
+        nc.vector.reciprocal(r[:], z[:])
+        neg_tp_u = big("neg_tp_u")
+        neg_b = col("neg_b")
+        nc.vector.scalar_tensor_tensor(neg_tp_u[:], neg_tp[:], 1.0, u[:], ALU.mult, ALU.mult, accum_out=neg_b[:])
+        neg_r_tz = col("neg_r_tz")
+        nc.scalar.activation(neg_r_tz[:], neg_tz[:], ACT.Identity, scale=r[:])
+        slope = big("slope")
+        nc.scalar.activation(slope[:], neg_v[:], ACT.Identity, scale=-1.0, bias=neg_r_tz[:])
+        neg_r_b = col("neg_r_b")
+        nc.scalar.activation(neg_r_b[:], neg_b[:], ACT.Identity, scale=r[:])
+        gain_r = col("gain_r")
+        nc.scalar.activation(gain_r[:], r[:], ACT.Identity, scale=GAIN)
+
+        neg_p_u = big("neg_p_u")
+        neg_c = col("neg_c")
+        nc.vector.scalar_tensor_tensor(neg_p_u[:], neg_p[:], r[:], u[:], ALU.mult, ALU.mult, accum_out=neg_c[:])
+        shift = col("shift")
+        nc.scalar.activation(shift[:], neg_c[:], ACT.Identity, scale=neg_r_tz[:], bias=neg_r_b[:])
+        k = big("k")
+        halves = (slice(0, SLOTS // 2), slice(SLOTS // 2, SLOTS))
+        for h in halves:
+            nc.vector.scalar_tensor_tensor(k[:, h], u[:, h], neg_c[:], slope[:, h], ALU.add, ALU.mult)
+        bracket = big("bracket")
+        for h in halves:
+            nc.vector.tensor_scalar(bracket[:, h], k[:, h], shift[:], gain_r[:], ALU.add, ALU.mult)
+        nc.vector.tensor_tensor(placed[:].indirect(offsets[:]), bracket[:], s[:], ALU.mult)
+
+        t0 = 0
+        for n, width in enumerate(OUT_CHUNKS):
+            cols = slice(t0, t0 + width)
+            result = held.tile([P, width], F32, name=f"result{n}")
+            nc.vector.tensor_tensor(result[:], placed[:, cols], base_sb[:, cols], ALU.add)
+            nc.sync.dma_start(out=out[:, cols], in_=result[:])
+            t0 = t0 + width

@@ -100,9 +100,12 @@ def tile_attend_hvsoftthreshold_s_kernel(tc, query, keys_words, keys_scales, th,
             nc.vector.tensor_copy(t[:], pool[:].indirect(offsets[:]))
             return t
 
-        def quantise(name, raw):
+        def interleave(name, raw, copy):
             grouped = held.tile([P, ROWS, PACK], BF16, name=name + "_bf16", align_bytes=64)
-            nc.scalar.copy(out=grouped[:], in_=raw[:].rearrange("p j w -> p w j"))
+            copy(out=grouped[:], in_=raw[:].rearrange("p j w -> p w j"))
+            return grouped
+
+        def quantise(name, grouped):
             words = held.tile([P, ROWS], U32, name=name + "_words", align_bytes=64)
             scales = held.tile([P, ROWS], U8, name=name + "_scales", align_bytes=64)
             nc.vector.quantize_mx(out=words[:].bitcast(FP8X4), scales=scales[:],
@@ -116,35 +119,36 @@ def tile_attend_hvsoftthreshold_s_kernel(tc, query, keys_words, keys_scales, th,
             return acc
 
         key_scales = gather("key_scales", key_scale_pool, U8)
-        query_mx = quantise("query", query_raw)
+        query_mx = quantise("query", interleave("query", query_raw, nc.scalar.copy))
         key_words = gather("key_words", key_word_pool, U32)
         a = product("a", query_mx, key_words, key_scales, tag="size_ps")
-        ta = product("ta", quantise("dquery", dquery_raw), key_words, key_scales)
-        val_scales = gather("val_scales", val_scale_pool, U8, tag="dquery_bf16")
+        ta = product("ta", quantise("dquery", interleave("dquery", dquery_raw, nc.scalar.copy)), key_words, key_scales)
+        val_scales = gather("val_scales", val_scale_pool, U8)
 
-        gout_mx = quantise("gout", gout_raw)
-        s = big("s", tag="gout_raw")
+        gout_bf16 = interleave("gout", gout_raw, nc.vector.tensor_copy)
+        s = held.tile([P, SLOTS], F32, name="s", tag="dquery_bf16", align_bytes=64)
         nc.scalar.activation(s[:], a[:], ACT.Sigmoid, bias=neg_th[:])
+        relu_x = big("relu_x")
+        sum_relu_x = col("sum_relu_x")
+        nc.scalar.activation(relu_x[:], a[:], ACT.Relu, bias=neg_th[:], accum_out=sum_relu_x[:])
         dist = big("dist")
         nc.scalar.activation(dist[:], s[:], ACT.Abs, bias=half[:], scale=-1.0)
         log_m = big("log_m")
         sum_log_m = col("sum_log_m")
         nc.scalar.activation(log_m[:], dist[:], ACT.Ln, bias=half[:], accum_out=sum_log_m[:])
-        relu_x = big("relu_x", tag="dist")
-        sum_relu_x = col("sum_relu_x")
-        nc.scalar.activation(relu_x[:], a[:], ACT.Relu, bias=neg_th[:], accum_out=sum_relu_x[:])
 
-        neg_tp = big("neg_tp", tag="val_scale_pool")
+        neg_tp = big("neg_tp", tag="gout_raw")
         neg_tz = col("neg_tz")
         nc.vector.scalar_tensor_tensor(neg_tp[:], ta[:], -1.0, s[:], ALU.mult, ALU.mult, accum_out=neg_tz[:])
 
+        gout_mx = quantise("gout", gout_bf16)
         val_words = gather("val_words", val_word_pool, U32)
         c0 = product("c0", gout_mx, val_words, val_scales)
         neg_v = big("neg_v", tag="val_word_pool")
         nc.vector.scalar_tensor_tensor(neg_v[:], s[:], 1.0, ta[:], ALU.subtract, ALU.mult)
         u = big("u")
         nc.vector.tensor_tensor(u[:], c0[:], size_rows[:], ALU.mult)
-        z = held.tile([P, 1], F32, name="z", tag="dquery_bf16", align_bytes=64)
+        z = held.tile([P, 1], F32, name="z", tag="val_scales", align_bytes=64)
         nc.vector.tensor_scalar(z[:], sum_relu_x[:], sum_log_m[:], reserve_sb[:], ALU.subtract, ALU.add)
         neg_p = held.tile([P, SLOTS], F32, name="neg_p", tag="val_words", align_bytes=64)
         nc.vector.tensor_tensor(neg_p[:], log_m[:], relu_x[:], ALU.subtract)

from contextlib import ExitStack

import concourse.mybir as mybir
from concourse.masks import make_identity

F32 = mybir.dt.float32
BF16 = mybir.dt.bfloat16
I32 = mybir.dt.int32
U32 = mybir.dt.uint32
U16 = mybir.dt.uint16
U8 = mybir.dt.uint8
FP8X4 = mybir.dt.float8_e4m3fn_x4
ALU = mybir.AluOpType
ACT = mybir.ActivationFunctionType

P = 128
PACK = 4
TOKENS = 2048
SLOTS = 512
ROWS = 128
GAIN = 512.0
OUT_CHUNKS = (256, 512, 512, 512, 256)

FLOPS = 3 * 2 * 512 * ROWS * SLOTS


def tile_attend_hvsoftthreshold_s_kernel(tc, query, keys_words, keys_scales, th, reserve, gout,
                                          vals_words, vals_scales, size, dquery, base, offs, out):
    nc = tc.nc
    with ExitStack() as ctx:
        held = ctx.enter_context(tc.tile_pool(name="held", bufs=1))
        psum = ctx.enter_context(tc.psum_pool(name="psum", bufs=1))

        def big(name, tag=None):
            return held.tile([P, SLOTS], F32, name=name, tag=tag or name)

        def col(name, tag=None):
            return held.tile([P, 1], F32, name=name, tag=tag or name)

        offsets = held.tile([P, SLOTS // 16], U16, name="offsets")
        nc.sync.dma_start(offsets[:], offs)

        def scale_pool(name, scales):
            t = held.tile([P, TOKENS], U8, name=name)
            nc.vector.memset(t[:].bitcast(I32), 0)
            for quad in range(4):
                nc.sync.dma_start(out=t[32 * quad:32 * quad + 4, :].bitcast(I32),
                                  in_=scales[0, 4 * quad:4 * quad + 4, :].bitcast(I32))
            return t

        def word_pool(name, words):
            t = held.tile([P, TOKENS], U32, name=name)
            nc.sync.dma_start(out=t[:].bitcast(I32), in_=words[0].rearrange("p n t -> p (n t)").bitcast(I32))
            return t

        def load_rows(name, x):
            t = held.tile([P, PACK, ROWS], F32, name=name)
            nc.sync.dma_start(out=t[:], in_=x.rearrange("(p j) w -> p j w", j=PACK))
            return t

        zero = col("zero")
        nc.gpsimd.memset(zero[:], 0.0)
        half = col("half")
        nc.scalar.activation(half[:], zero[:], ACT.Sigmoid)

        identity = held.tile([P, P], F32, name="identity")
        make_identity(nc, identity[:])
        size_cols = held.tile([P, PACK], F32, name="size_cols")
        nc.sync.dma_start(out=size_cols[:], in_=size.rearrange("o (p j) -> (o p) j", j=PACK))
        th_sb = col("th_sb")
        nc.gpsimd.dma_start(out=th_sb[:], in_=th)

        query_raw = load_rows("query_raw", query)
        key_scale_pool = scale_pool("key_scale_pool", keys_scales)
        key_word_pool = word_pool("key_word_pool", keys_words)
        dquery_raw = load_rows("dquery_raw", dquery)
        val_scale_pool = scale_pool("val_scale_pool", vals_scales)
        gout_raw = load_rows("gout_raw", gout)
        val_word_pool = word_pool("val_word_pool", vals_words)
        reserve_sb = col("reserve_sb")
        nc.sync.dma_start(out=reserve_sb[:], in_=reserve)
        base_sb = held.tile([P, TOKENS], F32, name="base_sb")
        nc.sync.dma_start(out=base_sb[:], in_=base)

        neg_th = col("neg_th")
        nc.gpsimd.tensor_scalar(neg_th[:], th_sb[:], -1.0, 0.0, ALU.mult, ALU.add)

        placed = held.tile([P, TOKENS], F32, name="placed")
        nc.vector.memset(placed[:], 0.0)

        size_ps = psum.tile([P, PACK, P], F32, name="size_ps")
        for j in range(PACK):
            nc.tensor.transpose(size_ps[:, j, :], size_cols[:, j:j + 1].to_broadcast([P, P]), identity[:])
        size_rows = big("size_rows")
        nc.scalar.copy(out=size_rows[:].rearrange("p (n j) -> p n j", j=PACK),
                       in_=size_ps[:].rearrange("p j n -> p n j"))

        def gather(name, pool, dtype, tag=None):
            t = held.tile([P, SLOTS], dtype, name=name, tag=tag or name, align_bytes=64)
            nc.vector.tensor_copy(t[:], pool[:].indirect(offsets[:]))
            return t

        def interleave(name, raw, copy):
            grouped = held.tile([P, ROWS, PACK], BF16, name=name + "_bf16", align_bytes=64)
            copy(out=grouped[:], in_=raw[:].rearrange("p j w -> p w j"))
            return grouped

        def quantise(name, grouped):
            words = held.tile([P, ROWS], U32, name=name + "_words", align_bytes=64)
            scales = held.tile([P, ROWS], U8, name=name + "_scales", align_bytes=64)
            nc.vector.quantize_mx(out=words[:].bitcast(FP8X4), scales=scales[:],
                                  in_=grouped[:].rearrange("p w j -> p (w j)"))
            return words, scales

        def product(name, rows, words, scales, tag=None):
            acc = psum.tile([P, SLOTS], F32, name=name, tag=tag or name)
            nc.tensor.matmul_mx(out=acc[:], lhsT=rows[0][:].bitcast(FP8X4), lhsT_scale=rows[1][:],
                                rhs=words[:].bitcast(FP8X4), rhs_scale=scales[:], start=True, stop=True)
            return acc

        key_scales = gather("key_scales", key_scale_pool, U8)
        query_mx = quantise("query", interleave("query", query_raw, nc.scalar.copy))
        key_words = gather("key_words", key_word_pool, U32)
        a = product("a", query_mx, key_words, key_scales, tag="size_ps")
        ta = product("ta", quantise("dquery", interleave("dquery", dquery_raw, nc.scalar.copy)), key_words, key_scales)
        val_scales = gather("val_scales", val_scale_pool, U8)

        gout_bf16 = interleave("gout", gout_raw, nc.vector.tensor_copy)
        s = held.tile([P, SLOTS], F32, name="s", tag="dquery_bf16", align_bytes=64)
        nc.scalar.activation(s[:], a[:], ACT.Sigmoid, bias=neg_th[:])
        relu_x = big("relu_x")
        sum_relu_x = col("sum_relu_x")
        nc.scalar.activation(relu_x[:], a[:], ACT.Relu, bias=neg_th[:], accum_out=sum_relu_x[:])
        dist = big("dist")
        nc.scalar.activation(dist[:], s[:], ACT.Abs, bias=half[:], scale=-1.0)
        log_m = big("log_m")
        sum_log_m = col("sum_log_m")
        nc.scalar.activation(log_m[:], dist[:], ACT.Ln, bias=half[:], accum_out=sum_log_m[:])

        neg_tp = big("neg_tp", tag="gout_raw")
        neg_tz = col("neg_tz")
        nc.vector.scalar_tensor_tensor(neg_tp[:], ta[:], -1.0, s[:], ALU.mult, ALU.mult, accum_out=neg_tz[:])

        gout_mx = quantise("gout", gout_bf16)
        val_words = gather("val_words", val_word_pool, U32)
        c0 = product("c0", gout_mx, val_words, val_scales)
        neg_v = big("neg_v", tag="val_word_pool")
        nc.vector.scalar_tensor_tensor(neg_v[:], s[:], 1.0, ta[:], ALU.subtract, ALU.mult)
        u = big("u")
        nc.vector.tensor_tensor(u[:], c0[:], size_rows[:], ALU.mult)
        z = held.tile([P, 1], F32, name="z", tag="val_scales", align_bytes=64)
        nc.vector.tensor_scalar(z[:], sum_relu_x[:], sum_log_m[:], reserve_sb[:], ALU.subtract, ALU.add)
        neg_p = held.tile([P, SLOTS], F32, name="neg_p", tag="val_words", align_bytes=64)
        nc.vector.tensor_tensor(neg_p[:], log_m[:], relu_x[:], ALU.subtract)
        r = col("r")
        nc.vector.reciprocal(r[:], z[:])
        neg_tp_u = big("neg_tp_u")
        neg_b = col("neg_b")
        nc.vector.scalar_tensor_tensor(neg_tp_u[:], neg_tp[:], 1.0, u[:], ALU.mult, ALU.mult, accum_out=neg_b[:])
        neg_r_tz = col("neg_r_tz")
        nc.scalar.activation(neg_r_tz[:], neg_tz[:], ACT.Identity, scale=r[:])
        slope = big("slope")
        nc.scalar.activation(slope[:], neg_v[:], ACT.Identity, scale=-1.0, bias=neg_r_tz[:])
        neg_r_b = col("neg_r_b")
        nc.scalar.activation(neg_r_b[:], neg_b[:], ACT.Identity, scale=r[:])
        gain_r = col("gain_r")
        nc.scalar.activation(gain_r[:], r[:], ACT.Identity, scale=GAIN)

        neg_p_u = big("neg_p_u")
        neg_c = col("neg_c")
        nc.vector.scalar_tensor_tensor(neg_p_u[:], neg_p[:], r[:], u[:], ALU.mult, ALU.mult, accum_out=neg_c[:])
        shift = col("shift")
        nc.scalar.activation(shift[:], neg_c[:], ACT.Identity, scale=neg_r_tz[:], bias=neg_r_b[:])
        k = big("k")
        halves = (slice(0, SLOTS // 2), slice(SLOTS // 2, SLOTS))
        for h in halves:
            nc.vector.scalar_tensor_tensor(k[:, h], u[:, h], neg_c[:], slope[:, h], ALU.add, ALU.mult)
        bracket = big("bracket")
        for h in halves:
            nc.vector.tensor_scalar(bracket[:, h], k[:, h], shift[:], gain_r[:], ALU.add, ALU.mult)
        nc.vector.tensor_tensor(placed[:].indirect(offsets[:]), bracket[:], s[:], ALU.mult)

        t0 = 0
        for n, width in enumerate(OUT_CHUNKS):
            cols = slice(t0, t0 + width)
            result = held.tile([P, width], F32, name=f"result{n}")
            nc.vector.tensor_tensor(result[:], placed[:, cols], base_sb[:, cols], ALU.add)
            nc.sync.dma_start(out=out[:, cols], in_=result[:])
            t0 = t0 + width
